import numpy as np
import ml_dtypes


def mxq(x, axis, fmt="e4m3"):
    dtype, down = {"e4m3": (ml_dtypes.float8_e4m3fn, 7), "e5m2": (ml_dtypes.float8_e5m2, 14)}[fmt]
    v = np.moveaxis(np.asarray(x, np.float32).astype(ml_dtypes.bfloat16).astype(np.float64), axis, -1)
    blocks = v.reshape(v.shape[:-1] + (-1, 32))
    amax = np.abs(blocks).max(-1, keepdims=True)
    byte = np.maximum(np.where(amax > 0, np.frexp(amax)[1] - 1 + 127, 0) - down, 1)
    scale = np.exp2(byte - 127.0)
    codes = (blocks / scale).astype(np.float32).astype(dtype).astype(np.float64)
    return np.moveaxis((codes * scale).reshape(v.shape), -1, axis)


WIDE = False


def mx_kscale(k):
    if not WIDE:
        return np.ones(k)
    levels = np.array([10, -10, 5, -5, 0])
    if k % 512:
        return np.exp2(np.random.permutation(np.resize(levels, k // 32))).repeat(32)
    a = np.empty((k // 512, 16))
    for p in range(k // 512):
        a[p, :8] = np.random.permutation(np.resize(levels, 8))
        for g in range(8):
            far = levels[np.abs(levels - a[p, g]) >= 10]
            a[p, g + 8] = far[np.random.randint(len(far))]
    return np.exp2(a.ravel()).repeat(32)


def f64(x):
    return np.asarray(x).astype(np.float64)


def striped(idx):
    return np.tile(np.asarray(idx).reshape(-1, 16).T, (8, 1)).astype(np.uint16)


def unstriped(offs):
    return offs[:16].T.reshape(-1).astype(np.int64)


E2M1 = np.array([0.0, 0.5, 1.0, 1.5, 2.0, 3.0, 4.0, 6.0, -0.0, -0.5, -1.0, -1.5, -2.0, -3.0, -4.0, -6.0])


def pack_weight(w, fmt):
    k, n = w.shape
    w = f64(np.asarray(w, np.float32).astype(ml_dtypes.bfloat16)).reshape(k // 32, 32, n)
    amax = np.abs(w).max(1)
    if fmt == "e4m3":
        byte = np.frexp(amax)[1] - 1 + 127 - 7
    else:
        mant, ex = np.frexp(amax / 6.0)
        byte = np.where(mant > 0.5, ex, ex - 1) + 127
    byte = np.clip(np.where(amax > 0, byte, 1), 1, 254)
    scaled = (w * np.exp2(127.0 - byte)[:, None, :]).reshape(k, n).astype(np.float32)
    by_word = np.ascontiguousarray(scaled.reshape(k // 512, 128, 4, n).transpose(0, 1, 3, 2))
    if fmt == "e4m3":
        words = by_word.astype(ml_dtypes.float8_e4m3fn).view(np.uint8)
    else:
        c = by_word.astype(ml_dtypes.float4_e2m1fn).view(np.uint8) & 0xF
        words = (c[..., 0::2] | (c[..., 1::2] << 4)).reshape(k // 512, 128, 2 * n)
    return np.ascontiguousarray(words), np.ascontiguousarray(byte.astype(np.uint8).reshape(k // 512, 16, n))


def unpack_weight(words, scales, fmt):
    g, _, n = scales.shape
    words = np.ascontiguousarray(words).reshape(g, 128, n, -1)
    if fmt == "e4m3":
        vals = words.view(ml_dtypes.float8_e4m3fn).astype(np.float64)
    else:
        nib = np.empty((g, 128, n, 4), np.uint8)
        nib[..., 0::2] = words & 0xF
        nib[..., 1::2] = words >> 4
        vals = E2M1[nib]
    vals = vals * np.repeat(np.exp2(scales.astype(np.float64) - 127.0), 8, axis=1)[..., None]
    return vals.transpose(0, 1, 3, 2).reshape(g * 512, n)


def sigmoid(v):
    return 1.0 / (1.0 + np.exp(-v))


D, T, I, Q, E, Z, X = 512, 2048, 512, 128, 512, 1024, 1024


def setup_inputs():
    n = np.random.standard_normal
    idx = np.random.permutation(T)[:I]
    idx2 = np.random.permutation(Z)[:I]
    idx3 = np.random.permutation(X)[:I]
    fd = mx_kscale(D)
    fi = mx_kscale(I)
    ti = np.ones(T)
    ti[idx] = fi
    ti3 = np.ones(X)
    ti3[idx3] = fi
    keysp = pack_weight(n((D, T)) / fd[:, None], "e4m3")
    return {
        "query": (n((D, Q)) * 1.0 / np.sqrt(D) * fd[:, None]).astype(np.float32),
        "query2": (n((D, Q)) * 1.0 / np.sqrt(D) * fd[:, None]).astype(np.float32),
        "keys_words": keysp[0],
        "keys_scales": keysp[1],
        "pages": (n((D, Z)) / fd[:, None]).astype(np.float32),
        "os": (np.random.uniform(0.02, 0.08, (1, I)) * fi).astype(np.float32),
        "os2": (np.random.uniform(0.02, 0.08, (1, I)) * fi).astype(np.float32),
        "vals": (n((E, T)) / ti).astype(np.float32),
        "vals2": (n((E, X)) / ti3).astype(np.float32),
        "offs": striped(idx),
        "offs2": striped(idx2),
        "offs3": striped(idx3),
    }


def reference(query, query2, keys_words, keys_scales, pages, os, os2, vals, vals2, offs, offs2, offs3):
    idx = unstriped(offs)
    idx2 = unstriped(offs2)
    idx3 = unstriped(offs3)
    keysu = unpack_weight(keys_words, keys_scales, "e4m3")
    queryq = mxq(f64(query), 0, "e4m3")
    keysidxg = keysu[:, idx]
    a = queryq.T @ keysidxg
    query2q = mxq(f64(query2), 0, "e4m3")
    pagesq = mxq(f64(pages), 0, "e4m3")
    h0 = query2q.T @ pagesq
    s = np.maximum(a, h0[:, idx2])
    w = sigmoid(s)
    wo1 = w * f64(os)
    wt1 = wo1.T
    wo2 = w * f64(os2)
    wt2 = wo2.T
    vt1 = f64(vals)[:, idx].T
    vt2 = f64(vals2)[:, idx3].T
    wt1q = mxq(wt1, 0, "e4m3")
    vt1q = mxq(vt1, 0, "e4m3")
    wt2q = mxq(wt2, 0, "e4m3")
    vt2q = mxq(vt2, 0, "e4m3")
    o = wt1q.T @ vt1q + wt2q.T @ vt2q
    return o

@@ -1,0 +1,172 @@
+from contextlib import ExitStack
+
+import concourse.mybir as mybir
+from concourse.masks import make_identity
+
+D, T, SLOTS, Q, E, Z, X = 512, 2048, 512, 128, 512, 1024, 1024
+FLOPS = 2 * D * Q * SLOTS + 2 * D * Q * Z + 2 * 2 * SLOTS * Q * E
+
+F32 = mybir.dt.float32
+BF16 = mybir.dt.bfloat16
+I32 = mybir.dt.int32
+U32 = mybir.dt.uint32
+U16 = mybir.dt.uint16
+U8 = mybir.dt.uint8
+FP8X4 = mybir.dt.float8_e4m3fn_x4
+ACT = mybir.ActivationFunctionType
+ALU = mybir.AluOpType
+
+P = 128
+PACK = 4
+BANK = 512
+E_BLOCKS = E // P
+LIST_COLS = SLOTS // 16
+
+
+def tile_attend_widelarger_twostores_lean_kernel(
+    tc, query, query2, keys_words, keys_scales, pages, factor1, factor2, vals, vals2, offs, offs2, offs3, out
+):
+    nc = tc.nc
+    with ExitStack() as ctx:
+        keep = ctx.enter_context(tc.tile_pool(name="keep", bufs=1))
+        psum = ctx.enter_context(tc.psum_pool(name="psum", bufs=1))
+
+        def sbuf(name, shape, dtype):
+            return keep.tile(shape, dtype, name=name, align_bytes=64)
+
+        def interleave(dst, src):
+            nc.vector.tensor_copy(
+                out=dst.rearrange("p (c i) t -> p c t i", i=4),
+                in_=src.rearrange("p t (c i) -> p c t i", i=4),
+            )
+
+        def quantize(name, grouped, width):
+            codes = sbuf(name + "_codes", [P, width], U32)
+            scales = sbuf(name + "_scales", [P, width], U8)
+            nc.vector.quantize_mx(out=codes[:].bitcast(FP8X4), scales=scales[:], in_=grouped)
+            return codes, scales
+
+        def product(acc, lhs, lhs_cols, rhs, start, stop):
+            nc.tensor.matmul_mx(
+                out=acc,
+                lhsT=lhs[0][:, lhs_cols].bitcast(FP8X4),
+                lhsT_scale=lhs[1][:, lhs_cols],
+                rhs=rhs[0][:].bitcast(FP8X4),
+                rhs_scale=rhs[1][:],
+                start=start,
+                stop=stop,
+            )
+
+        pages_by_k = pages.rearrange("(p t) z -> p t z", t=PACK)
+        pages_raw = []
+        for h in range(Z // BANK):
+            raw = sbuf("pages_raw%d" % h, [P, PACK, BANK], F32)
+            nc.sync.dma_start(out=raw[:], in_=pages_by_k[:, :, h * BANK : (h + 1) * BANK])
+            pages_raw.append(raw)
+        query2_raw = sbuf("query2_raw", [P, PACK, Q], F32)
+        nc.sync.dma_start(out=query2_raw[:], in_=query2.rearrange("(p t) q -> p t q", t=PACK))
+        query_raw = sbuf("query_raw", [P, PACK, Q], F32)
+        nc.sync.dma_start(out=query_raw[:], in_=query.rearrange("(p t) q -> p t q", t=PACK))
+        page_list = sbuf("page_list", [P, LIST_COLS], U16)
+        nc.sync.dma_start(page_list[:], offs2)
+        token_list = sbuf("token_list", [P, LIST_COLS], U16)
+        nc.sync.dma_start(token_list[:], offs)
+        column_list = sbuf("column_list", [P, LIST_COLS], U16)
+        nc.sync.dma_start(column_list[:], offs3)
+        key_words = sbuf("key_words", [P, T], U32)
+        nc.sync.dma_start(
+            out=key_words[:].bitcast(I32), in_=keys_words[0].rearrange("p n t -> p (n t)").bitcast(I32)
+        )
+        stores = []
+        for j in range(E_BLOCKS):
+            rows = slice(j * P, (j + 1) * P)
+            store2 = sbuf("store2_%d" % j, [P, X], F32)
+            nc.sync.dma_start(out=store2[:], in_=vals2[rows, :])
+            store1 = sbuf("store1_%d" % j, [P, T], F32)
+            nc.sync.dma_start(out=store1[:], in_=vals[rows, :])
+            stores.append((store2, store1))
+
+        key_scales = sbuf("key_scales", [P, T], U8)
+        nc.vector.memset(key_scales[:].bitcast(I32), 0)
+        for quad in range(4):
+            nc.gpsimd.dma_start(
+                out=key_scales[32 * quad : 32 * quad + 4, :].bitcast(I32),
+                in_=keys_scales[0, 4 * quad : 4 * quad + 4, :].bitcast(I32),
+            )
+        factors = []
+        for n, factor in enumerate((factor2, factor1)):
+            column = sbuf("factor%d" % n, [P, PACK], F32)
+            nc.gpsimd.dma_start(out=column[:], in_=factor[0].rearrange("(p t) -> p t", t=PACK))
+            factors.append(column)
+        identity = sbuf("identity", [P, P], F32)
+        make_identity(nc, identity[:])
+
+        pages_mx = []
+        for h in range(Z // BANK):
+            grouped = sbuf("pages_grouped%d" % h, [P, BANK, PACK], BF16)
+            interleave(grouped[:], pages_raw[h][:])
+            pages_mx.append(quantize("pages%d" % h, grouped[:].rearrange("p z t -> p (z t)"), BANK))
+        queries_grouped = sbuf("queries_grouped", [P, 2 * Q, PACK], BF16)
+        interleave(queries_grouped[:, 0:Q, :], query2_raw[:])
+        interleave(queries_grouped[:, Q : 2 * Q, :], query_raw[:])
+        queries_mx = quantize("queries", queries_grouped[:].rearrange("p q t -> p (q t)"), 2 * Q)
+
+        page_scores = sbuf("page_scores", [P, Z], F32)
+        for h in range(Z // BANK):
+            bank = psum.tile([P, BANK], F32, name="page_bank%d" % h)
+            product(bank[:], queries_mx, slice(0, Q), pages_mx[h], True, True)
+            nc.scalar.copy(out=page_scores[:, h * BANK : (h + 1) * BANK], in_=bank[:])
+        picked_page_scores = sbuf("picked_page_scores", [P, SLOTS], F32)
+        nc.scalar.activation(picked_page_scores[:], page_scores[:].indirect(page_list[:]), ACT.Copy)
+
+        picked_words = sbuf("picked_words", [P, SLOTS], U32)
+        nc.vector.tensor_copy(picked_words[:], key_words[:].indirect(token_list[:]))
+        picked_scales = sbuf("picked_scales", [P, SLOTS], U8)
+        nc.vector.tensor_copy(picked_scales[:], key_scales[:].indirect(token_list[:]))
+        token_bank = psum.tile([P, SLOTS], F32, name="token_bank")
+        product(token_bank[:], queries_mx, slice(Q, 2 * Q), (picked_words, picked_scales), True, True)
+
+        scores = sbuf("scores", [P, SLOTS], F32)
+        nc.vector.tensor_tensor(scores[:], token_bank[:], picked_page_scores[:], ALU.max)
+        weights = sbuf("weights", [P, SLOTS], F32)
+        nc.scalar.activation(weights[:], scores[:], ACT.Sigmoid)
+        weight_bank = psum.tile([P, PACK, Q], F32, name="weight_bank")
+        for t in range(PACK):
+            nc.tensor.transpose(weight_bank[:, t, :], weights[:, t:SLOTS:PACK], identity[:])
+        weights_grouped = sbuf("weights_grouped", [P, 2, Q, PACK], BF16)
+        for n in range(2):
+            nc.vector.tensor_tensor(
+                weights_grouped[:, n, :, :],
+                weight_bank[:].rearrange("p t q -> p q t"),
+                factors[n][:].unsqueeze(1).to_broadcast([P, Q, PACK]),
+                ALU.mult,
+            )
+        weights_mx = quantize("weights", weights_grouped[:].rearrange("p n q t -> p (n q t)"), 2 * Q)
+
+        lists = (column_list, token_list)
+        half = SLOTS // 2
+        for j in range(E_BLOCKS):
+            values_mx = []
+            for n in range(2):
+                name = "values%d_%d" % (j, n)
+                picked = sbuf(name + "_picked", [P, SLOTS], BF16)
+                window = stores[j][n]
+                nc.vector.tensor_copy(picked[:, 0:half], window[:].indirect(lists[n][:, 0 : LIST_COLS // 2]))
+                nc.scalar.activation(
+                    picked[:, half:SLOTS], window[:].indirect(lists[n][:, LIST_COLS // 2 : LIST_COLS]), ACT.Copy
+                )
+                pairs = picked[:].bitcast(F32)
+                turned = psum.tile([P, 2, P], F32, name=name + "_turned", tag="turned", bufs=2)
+                for u in range(2):
+                    nc.tensor.transpose(turned[:, u, :], pairs[:, u : SLOTS // 2 : 2], identity[:])
+                grouped = sbuf(name + "_grouped", [P, P, PACK], BF16)
+                nc.scalar.copy(
+                    out=grouped[:].bitcast(F32), in_=turned[:].rearrange("p u e -> p e u")
+                )
+                values_mx.append(quantize(name, grouped[:].rearrange("p e t -> p (e t)"), P))
+            acc = psum.tile([P, P], F32, name="acc%d" % j, tag="acc", bufs=2)
+            for n in range(2):
+                product(acc[:], weights_mx, slice(n * Q, (n + 1) * Q), values_mx[n], n == 0, n == 1)
+            result = sbuf("result%d" % j, [P, P], F32)
+            nc.scalar.copy(out=result[:], in_=acc[:])
+            nc.sync.dma_start(out=out[:, j * P : (j + 1) * P], in_=result[:])

@@ -21,6 +21,8 @@ PACK = 4
 BANK = 512
 E_BLOCKS = E // P
 LIST_COLS = SLOTS // 16
+VEC_COLS = 320
+LAST_VEC_LIST_COLS = 18
 
 
 def tile_attend_widelarger_twostores_lean_kernel(
@@ -29,16 +31,19 @@ def tile_attend_widelarger_twostores_lean_kernel(
     nc = tc.nc
     with ExitStack() as ctx:
         keep = ctx.enter_context(tc.tile_pool(name="keep", bufs=1))
+        shared = ctx.enter_context(tc.tile_pool(name="shared", bufs=1))
         psum = ctx.enter_context(tc.psum_pool(name="psum", bufs=1))
 
         def sbuf(name, shape, dtype):
-            return keep.tile(shape, dtype, name=name, align_bytes=64)
+            return keep.tile(shape, dtype, name=name, tag=name, align_bytes=64)
 
-        def interleave(dst, src):
-            nc.vector.tensor_copy(
-                out=dst.rearrange("p (c i) t -> p c t i", i=4),
-                in_=src.rearrange("p t (c i) -> p c t i", i=4),
-            )
+        def load(name, shape, dtype, source):
+            tile = sbuf(name, shape, dtype)
+            nc.sync.dma_start(tile[:], source)
+            return tile
+
+        def by_fours(dst, src):
+            return dst.rearrange("p (c i) t -> p c t i", i=4), src.rearrange("p t (c i) -> p c t i", i=4)
 
         def quantize(name, grouped, width):
             codes = sbuf(name + "_codes", [P, width], U32)
@@ -46,94 +51,97 @@ def tile_attend_widelarger_twostores_lean_kernel(
             nc.vector.quantize_mx(out=codes[:].bitcast(FP8X4), scales=scales[:], in_=grouped)
             return codes, scales
 
-        def product(acc, lhs, lhs_cols, rhs, start, stop):
+        def product(acc, lhs, lhs_cols, rhs, rhs_cols, start, stop):
             nc.tensor.matmul_mx(
                 out=acc,
                 lhsT=lhs[0][:, lhs_cols].bitcast(FP8X4),
                 lhsT_scale=lhs[1][:, lhs_cols],
-                rhs=rhs[0][:].bitcast(FP8X4),
-                rhs_scale=rhs[1][:],
+                rhs=rhs[0][:, rhs_cols].bitcast(FP8X4),
+                rhs_scale=rhs[1][:, rhs_cols],
                 start=start,
                 stop=stop,
             )
 
+        key_scales = sbuf("key_scales", [P, T], U8)
+        nc.gpsimd.memset(key_scales[:].bitcast(I32), 0)
+        identity = sbuf("identity", [P, P], F32)
+        make_identity(nc, identity[:])
+
         pages_by_k = pages.rearrange("(p t) z -> p t z", t=PACK)
-        pages_raw = []
-        for h in range(Z // BANK):
-            raw = sbuf("pages_raw%d" % h, [P, PACK, BANK], F32)
-            nc.sync.dma_start(out=raw[:], in_=pages_by_k[:, :, h * BANK : (h + 1) * BANK])
-            pages_raw.append(raw)
-        query2_raw = sbuf("query2_raw", [P, PACK, Q], F32)
-        nc.sync.dma_start(out=query2_raw[:], in_=query2.rearrange("(p t) q -> p t q", t=PACK))
-        query_raw = sbuf("query_raw", [P, PACK, Q], F32)
-        nc.sync.dma_start(out=query_raw[:], in_=query.rearrange("(p t) q -> p t q", t=PACK))
-        page_list = sbuf("page_list", [P, LIST_COLS], U16)
-        nc.sync.dma_start(page_list[:], offs2)
-        token_list = sbuf("token_list", [P, LIST_COLS], U16)
-        nc.sync.dma_start(token_list[:], offs)
-        column_list = sbuf("column_list", [P, LIST_COLS], U16)
-        nc.sync.dma_start(column_list[:], offs3)
+        query2_raw = load("query2_raw", [P, PACK, Q], F32, query2.rearrange("(p t) q -> p t q", t=PACK))
+        pages_raw = [
+            load("pages_raw%d" % h, [P, PACK, BANK], F32, pages_by_k[:, :, h * BANK : (h + 1) * BANK])
+            for h in range(Z // BANK)
+        ]
+        token_list = load("token_list", [P, LIST_COLS], U16, offs)
+        query_raw = load("query_raw", [P, PACK, Q], F32, query.rearrange("(p t) q -> p t q", t=PACK))
+        for row in range(4):
+            nc.sync.dma_start(
+                out=key_scales[row:P:32, :].bitcast(I32), in_=keys_scales[0, row:16:4, :].bitcast(I32)
+            )
         key_words = sbuf("key_words", [P, T], U32)
         nc.sync.dma_start(
             out=key_words[:].bitcast(I32), in_=keys_words[0].rearrange("p n t -> p (n t)").bitcast(I32)
         )
+        page_list = load("page_list", [P, LIST_COLS], U16, offs2)
+        column_list = load("column_list", [P, LIST_COLS], U16, offs3)
         stores = []
+        factors = []
         for j in range(E_BLOCKS):
             rows = slice(j * P, (j + 1) * P)
-            store2 = sbuf("store2_%d" % j, [P, X], F32)
-            nc.sync.dma_start(out=store2[:], in_=vals2[rows, :])
-            store1 = sbuf("store1_%d" % j, [P, T], F32)
-            nc.sync.dma_start(out=store1[:], in_=vals[rows, :])
+            store2 = load("store2_%d" % j, [P, X], F32, vals2[rows, :])
+            if j < E_BLOCKS - 1:
+                store1 = load("store1_%d" % j, [P, T], F32, vals[rows, :])
+            else:
+                store1 = shared.tile([P, T], F32, name="last_store1", align_bytes=64, offset=0)
+                nc.sync.dma_start(store1[:], vals[rows, :])
             stores.append((store2, store1))
+            if j == 0:
+                for n, factor in enumerate((factor2, factor1)):
+                    factors.append(load("factor%d" % n, [P, PACK], F32, factor[0].rearrange("(p t) -> p t", t=PACK)))
 
-        key_scales = sbuf("key_scales", [P, T], U8)
-        nc.vector.memset(key_scales[:].bitcast(I32), 0)
-        for quad in range(4):
-            nc.gpsimd.dma_start(
-                out=key_scales[32 * quad : 32 * quad + 4, :].bitcast(I32),
-                in_=keys_scales[0, 4 * quad : 4 * quad + 4, :].bitcast(I32),
-            )
-        factors = []
-        for n, factor in enumerate((factor2, factor1)):
-            column = sbuf("factor%d" % n, [P, PACK], F32)
-            nc.gpsimd.dma_start(out=column[:], in_=factor[0].rearrange("(p t) -> p t", t=PACK))
-            factors.append(column)
-        identity = sbuf("identity", [P, P], F32)
-        make_identity(nc, identity[:])
+        def quantize_queries(name, raw):
+            grouped = sbuf(name + "_grouped", [P, Q, PACK], BF16)
+            nc.scalar.copy(*by_fours(grouped[:], raw[:]))
+            return quantize(name, grouped[:].rearrange("p q t -> p (q t)"), Q)
 
-        pages_mx = []
-        for h in range(Z // BANK):
-            grouped = sbuf("pages_grouped%d" % h, [P, BANK, PACK], BF16)
-            interleave(grouped[:], pages_raw[h][:])
-            pages_mx.append(quantize("pages%d" % h, grouped[:].rearrange("p z t -> p (z t)"), BANK))
-        queries_grouped = sbuf("queries_grouped", [P, 2 * Q, PACK], BF16)
-        interleave(queries_grouped[:, 0:Q, :], query2_raw[:])
-        interleave(queries_grouped[:, Q : 2 * Q, :], query_raw[:])
-        queries_mx = quantize("queries", queries_grouped[:].rearrange("p q t -> p (q t)"), 2 * Q)
-
+        query2_mx = quantize_queries("query2", query2_raw)
         page_scores = sbuf("page_scores", [P, Z], F32)
-        for h in range(Z // BANK):
+
+        def score_pages(h):
+            grouped = sbuf("pages_grouped%d" % h, [P, BANK, PACK], BF16)
+            nc.vector.tensor_copy(*by_fours(grouped[:, 0:VEC_COLS, :], pages_raw[h][:, :, 0:VEC_COLS]))
+            nc.scalar.copy(*by_fours(grouped[:, VEC_COLS:BANK, :], pages_raw[h][:, :, VEC_COLS:BANK]))
+            pages_mx = quantize("pages%d" % h, grouped[:].rearrange("p z t -> p (z t)"), BANK)
             bank = psum.tile([P, BANK], F32, name="page_bank%d" % h)
-            product(bank[:], queries_mx, slice(0, Q), pages_mx[h], True, True)
+            product(bank[:], query2_mx, slice(0, Q), pages_mx, slice(0, BANK), True, True)
             nc.scalar.copy(out=page_scores[:, h * BANK : (h + 1) * BANK], in_=bank[:])
+
+        score_pages(0)
+        score_pages(1)
+        query_mx = quantize_queries("query", query_raw)
+        picked_scales = sbuf("picked_scales", [P, SLOTS], U8)
+        nc.vector.tensor_copy(picked_scales[:], key_scales[:].indirect(token_list[:]))
+        picked_words = sbuf("picked_words", [P, SLOTS], U32)
+        nc.vector.tensor_copy(picked_words[:], key_words[:].indirect(token_list[:]))
         picked_page_scores = sbuf("picked_page_scores", [P, SLOTS], F32)
         nc.scalar.activation(picked_page_scores[:], page_scores[:].indirect(page_list[:]), ACT.Copy)
 
-        picked_words = sbuf("picked_words", [P, SLOTS], U32)
-        nc.vector.tensor_copy(picked_words[:], key_words[:].indirect(token_list[:]))
-        picked_scales = sbuf("picked_scales", [P, SLOTS], U8)
-        nc.vector.tensor_copy(picked_scales[:], key_scales[:].indirect(token_list[:]))
         token_bank = psum.tile([P, SLOTS], F32, name="token_bank")
-        product(token_bank[:], queries_mx, slice(Q, 2 * Q), (picked_words, picked_scales), True, True)
+        product(token_bank[:], query_mx, slice(0, Q), (picked_words, picked_scales), slice(0, SLOTS), True, True)
 
-        scores = sbuf("scores", [P, SLOTS], F32)
+        scores = sbuf("store2_0", [P, SLOTS], F32)
         nc.vector.tensor_tensor(scores[:], token_bank[:], picked_page_scores[:], ALU.max)
-        weights = sbuf("weights", [P, SLOTS], F32)
-        nc.scalar.activation(weights[:], scores[:], ACT.Sigmoid)
+        weights = sbuf("weights", [P, PACK, P], F32)
+        nc.scalar.activation(
+            weights[:].rearrange("q t (c i) -> q c t i", i=4),
+            scores[:].rearrange("q (c i t) -> q c t i", i=4, t=PACK),
+            ACT.Sigmoid,
+        )
         weight_bank = psum.tile([P, PACK, Q], F32, name="weight_bank")
         for t in range(PACK):
-            nc.tensor.transpose(weight_bank[:, t, :], weights[:, t:SLOTS:PACK], identity[:])
-        weights_grouped = sbuf("weights_grouped", [P, 2, Q, PACK], BF16)
+            nc.tensor.transpose(weight_bank[:, t, :], weights[:, t, :], identity[:])
+        weights_grouped = sbuf("store2_1", [P, 2, Q, PACK], BF16)
         for n in range(2):
             nc.vector.tensor_tensor(
                 weights_grouped[:, n, :, :],
@@ -143,30 +151,69 @@ def tile_attend_widelarger_twostores_lean_kernel(
             )
         weights_mx = quantize("weights", weights_grouped[:].rearrange("p n q t -> p (n q t)"), 2 * Q)
 
-        lists = (column_list, token_list)
-        half = SLOTS // 2
-        for j in range(E_BLOCKS):
-            values_mx = []
-            for n in range(2):
-                name = "values%d_%d" % (j, n)
-                picked = sbuf(name + "_picked", [P, SLOTS], BF16)
-                window = stores[j][n]
-                nc.vector.tensor_copy(picked[:, 0:half], window[:].indirect(lists[n][:, 0 : LIST_COLS // 2]))
-                nc.scalar.activation(
-                    picked[:, half:SLOTS], window[:].indirect(lists[n][:, LIST_COLS // 2 : LIST_COLS]), ACT.Copy
-                )
-                pairs = picked[:].bitcast(F32)
-                turned = psum.tile([P, 2, P], F32, name=name + "_turned", tag="turned", bufs=2)
-                for u in range(2):
-                    nc.tensor.transpose(turned[:, u, :], pairs[:, u : SLOTS // 2 : 2], identity[:])
-                grouped = sbuf(name + "_grouped", [P, P, PACK], BF16)
-                nc.scalar.copy(
-                    out=grouped[:].bitcast(F32), in_=turned[:].rearrange("p u e -> p e u")
-                )
-                values_mx.append(quantize(name, grouped[:].rearrange("p e t -> p (e t)"), P))
-            acc = psum.tile([P, P], F32, name="acc%d" % j, tag="acc", bufs=2)
-            for n in range(2):
-                product(acc[:], weights_mx, slice(n * Q, (n + 1) * Q), values_mx[n], n == 0, n == 1)
-            result = sbuf("result%d" % j, [P, P], F32)
-            nc.scalar.copy(out=result[:], in_=acc[:])
-            nc.sync.dma_start(out=out[:, j * P : (j + 1) * P], in_=result[:])
+        last = E_BLOCKS - 1
+
+        def turn(name, picked, words, copy):
+            pairs = picked[:].bitcast(F32)
+            turned = psum.tile([P, 2, P], F32, name=name + "_turned", tag="turned", bufs=2)
+            for u in range(2):
+                nc.tensor.transpose(turned[:, u, :], pairs[:, u : SLOTS // 2 : 2], identity[:])
+            copy(out=words.bitcast(F32), in_=turned[:].rearrange("p u e -> p e u"))
+
+        early_values2 = []
+        early_grouped1 = sbuf("early_grouped1", [P, last, P, PACK], BF16)
+        for j in range(last):
+            picked2 = sbuf("picked2_%d" % j, [P, SLOTS], BF16)
+            nc.vector.tensor_copy(picked2[:], stores[j][0][:].indirect(column_list[:]))
+            grouped2 = sbuf("grouped2_%d" % j, [P, P, PACK], BF16)
+            turn("values2_%d" % j, picked2, grouped2[:], nc.vector.tensor_copy)
+            early_values2.append(quantize("values2_%d" % j, grouped2[:].rearrange("p e t -> p (e t)"), P))
+            picked1 = sbuf("picked1_%d" % j, [P, SLOTS], BF16)
+            nc.scalar.activation(picked1[:], stores[j][1][:].indirect(token_list[:]), ACT.Copy)
+            turn("values1_%d" % j, picked1, early_grouped1[:, j, :, :], nc.scalar.copy)
+
+        last_grouped2 = sbuf("last_grouped2", [P, P, PACK], BF16)
+        last_grouped1 = sbuf("last_grouped1", [P, P, PACK], BF16)
+        picked2 = sbuf("picked2_%d" % last, [P, SLOTS], BF16)
+        nc.vector.tensor_copy(picked2[:], stores[last][0][:].indirect(column_list[:]))
+        turn("values2_%d" % last, picked2, last_grouped2[:], nc.scalar.copy)
+
+        early_codes1 = sbuf("store2_%d" % last, [P, last * P], U32)
+        early_scales1 = sbuf("early_scales1", [P, last * P], U8)
+        for first, stop in ((0, last - 1), (last - 1, last)):
+            nc.vector.quantize_mx(
+                out=early_codes1[:, first * P : stop * P].bitcast(FP8X4),
+                scales=early_scales1[:, first * P : stop * P],
+                in_=early_grouped1[:, first:stop, :, :].rearrange("p j e t -> p (j e t)"),
+            )
+        early_bank = psum.tile([P, last * P], F32, name="early_bank")
+        for j in range(last):
+            cols = slice(j * P, (j + 1) * P)
+            product(early_bank[:, cols], weights_mx, slice(Q, 2 * Q), (early_codes1, early_scales1), cols, True, False)
+            product(early_bank[:, cols], weights_mx, slice(0, Q), early_values2[j], slice(0, P), False, True)
+
+        picked1 = sbuf("picked1_%d" % last, [P, SLOTS], BF16)
+        cut = 16 * LAST_VEC_LIST_COLS
+        window = stores[last][1]
+        nc.vector.tensor_copy(picked1[:, 0:cut], window[:].indirect(token_list[:, 0:LAST_VEC_LIST_COLS]))
+        nc.scalar.activation(
+            picked1[:, cut:SLOTS], window[:].indirect(token_list[:, LAST_VEC_LIST_COLS:LIST_COLS]), ACT.Copy
+        )
+        turn("values1_%d" % last, picked1, last_grouped1[:], nc.scalar.copy)
+
+        last_codes2 = shared.tile([P, P], U32, name="last_codes2", align_bytes=64, offset=0)
+        last_scales2 = sbuf("last_scales2", [P, P], U8)
+        nc.vector.quantize_mx(
+            out=last_codes2[:].bitcast(FP8X4), scales=last_scales2[:], in_=last_grouped2[:].rearrange("p e t -> p (e t)")
+        )
+        early_result = shared.tile([P, last * P], F32, name="early_result", align_bytes=64, offset=4 * P)
+        nc.vector.tensor_copy(out=early_result[:], in_=early_bank[:])
+        nc.sync.dma_start(out=out[:, 0 : last * P], in_=early_result[:])
+
+        last_values1 = quantize("last_values1", last_grouped1[:].rearrange("p e t -> p (e t)"), P)
+        last_bank = psum.tile([P, P], F32, name="last_bank")
+        product(last_bank[:], weights_mx, slice(0, Q), (last_codes2, last_scales2), slice(0, P), True, False)
+        product(last_bank[:], weights_mx, slice(Q, 2 * Q), last_values1, slice(0, P), False, True)
+        last_result = sbuf("last_result", [P, P], F32)
+        nc.scalar.copy(out=last_result[:], in_=last_bank[:])
+        nc.scalar.dma_start(out=out[:, last * P : E], in_=last_result[:])

@@ -160,38 +160,32 @@ def tile_attend_widelarger_twostores_lean_kernel(
                 nc.tensor.transpose(turned[:, u, :], pairs[:, u : SLOTS // 2 : 2], identity[:])
             copy(out=words.bitcast(F32), in_=turned[:].rearrange("p u e -> p e u"))
 
-        early_values2 = []
-        early_grouped1 = sbuf("early_grouped1", [P, last, P, PACK], BF16)
-        for j in range(last):
-            picked2 = sbuf("picked2_%d" % j, [P, SLOTS], BF16)
-            nc.vector.tensor_copy(picked2[:], stores[j][0][:].indirect(column_list[:]))
-            grouped2 = sbuf("grouped2_%d" % j, [P, P, PACK], BF16)
-            turn("values2_%d" % j, picked2, grouped2[:], nc.vector.tensor_copy)
-            early_values2.append(quantize("values2_%d" % j, grouped2[:].rearrange("p e t -> p (e t)"), P))
-            picked1 = sbuf("picked1_%d" % j, [P, SLOTS], BF16)
-            nc.scalar.activation(picked1[:], stores[j][1][:].indirect(token_list[:]), ACT.Copy)
-            turn("values1_%d" % j, picked1, early_grouped1[:, j, :, :], nc.scalar.copy)
+        def pick_store2(j):
+            picked = sbuf("picked2_%d" % j, [P, SLOTS], BF16)
+            nc.vector.tensor_copy(picked[:], stores[j][0][:].indirect(column_list[:]))
+            return picked
 
-        last_grouped2 = sbuf("last_grouped2", [P, P, PACK], BF16)
-        last_grouped1 = sbuf("last_grouped1", [P, P, PACK], BF16)
-        picked2 = sbuf("picked2_%d" % last, [P, SLOTS], BF16)
-        nc.vector.tensor_copy(picked2[:], stores[last][0][:].indirect(column_list[:]))
-        turn("values2_%d" % last, picked2, last_grouped2[:], nc.scalar.copy)
-
-        early_codes1 = sbuf("store2_%d" % last, [P, last * P], U32)
-        early_scales1 = sbuf("early_scales1", [P, last * P], U8)
-        for first, stop in ((0, last - 1), (last - 1, last)):
-            nc.vector.quantize_mx(
-                out=early_codes1[:, first * P : stop * P].bitcast(FP8X4),
-                scales=early_scales1[:, first * P : stop * P],
-                in_=early_grouped1[:, first:stop, :, :].rearrange("p j e t -> p (j e t)"),
-            )
         early_bank = psum.tile([P, last * P], F32, name="early_bank")
-        for j in range(last):
-            cols = slice(j * P, (j + 1) * P)
-            product(early_bank[:, cols], weights_mx, slice(Q, 2 * Q), (early_codes1, early_scales1), cols, True, False)
-            product(early_bank[:, cols], weights_mx, slice(0, Q), early_values2[j], slice(0, P), False, True)
+        for blocks in ((0, 1), (2,)):
+            grouped = sbuf("grouped%d" % blocks[0], [P, len(blocks), 2, P, PACK], BF16)
+            for place, j in enumerate(blocks):
+                turn("values2_%d" % j, pick_store2(j), grouped[:, place, 0, :, :], nc.vector.tensor_copy)
+                picked1 = sbuf("picked1_%d" % j, [P, SLOTS], BF16)
+                nc.scalar.activation(picked1[:], stores[j][1][:].indirect(token_list[:]), ACT.Copy)
+                turn("values1_%d" % j, picked1, grouped[:, place, 1, :, :], nc.scalar.copy)
+            width = len(blocks) * 2 * P
+            codes = sbuf("store2_%d" % (blocks[-1] + 1), [P, width], U32)
+            scales = sbuf("scales%d" % blocks[0], [P, width], U8)
+            nc.vector.quantize_mx(
+                out=codes[:].bitcast(FP8X4), scales=scales[:], in_=grouped[:].rearrange("p j n e t -> p (j n e t)")
+            )
+            for place, j in enumerate(blocks):
+                for n in range(2):
+                    cols = slice((2 * place + n) * P, (2 * place + n + 1) * P)
+                    acc = early_bank[:, j * P : (j + 1) * P]
+                    product(acc, weights_mx, slice(n * Q, (n + 1) * Q), (codes, scales), cols, n == 0, n == 1)
 
+        picked2 = pick_store2(last)
         picked1 = sbuf("picked1_%d" % last, [P, SLOTS], BF16)
         cut = 16 * LAST_VEC_LIST_COLS
         window = stores[last][1]
@@ -199,20 +193,18 @@ def tile_attend_widelarger_twostores_lean_kernel(
         nc.scalar.activation(
             picked1[:, cut:SLOTS], window[:].indirect(token_list[:, LAST_VEC_LIST_COLS:LIST_COLS]), ACT.Copy
         )
-        turn("values1_%d" % last, picked1, last_grouped1[:], nc.scalar.copy)
-
-        last_codes2 = shared.tile([P, P], U32, name="last_codes2", align_bytes=64, offset=0)
-        last_scales2 = sbuf("last_scales2", [P, P], U8)
-        nc.vector.quantize_mx(
-            out=last_codes2[:].bitcast(FP8X4), scales=last_scales2[:], in_=last_grouped2[:].rearrange("p e t -> p (e t)")
-        )
-        early_result = shared.tile([P, last * P], F32, name="early_result", align_bytes=64, offset=4 * P)
-        nc.vector.tensor_copy(out=early_result[:], in_=early_bank[:])
+        last_grouped2 = shared.tile([P, P, PACK], BF16, name="last_grouped2", align_bytes=64, offset=0)
+        turn("values2_%d" % last, picked2, last_grouped2[:], nc.vector.tensor_copy)
+        last_values2 = quantize("last_values2", last_grouped2[:].rearrange("p e t -> p (e t)"), P)
+        early_result = shared.tile([P, last * P], F32, name="early_result", align_bytes=64, offset=2 * PACK * P)
+        nc.scalar.copy(out=early_result[:], in_=early_bank[:])
         nc.sync.dma_start(out=out[:, 0 : last * P], in_=early_result[:])
 
+        last_grouped1 = sbuf("last_grouped1", [P, P, PACK], BF16)
+        turn("values1_%d" % last, picked1, last_grouped1[:], nc.scalar.copy)
         last_values1 = quantize("last_values1", last_grouped1[:].rearrange("p e t -> p (e t)"), P)
         last_bank = psum.tile([P, P], F32, name="last_bank")
-        product(last_bank[:], weights_mx, slice(0, Q), (last_codes2, last_scales2), slice(0, P), True, False)
+        product(last_bank[:], weights_mx, slice(0, Q), last_values2, slice(0, P), True, False)
         product(last_bank[:], weights_mx, slice(Q, 2 * Q), last_values1, slice(0, P), False, True)
         last_result = sbuf("last_result", [P, P], F32)
         nc.scalar.copy(out=last_result[:], in_=last_bank[:])

from contextlib import ExitStack

import concourse.mybir as mybir
from concourse.masks import make_identity

D, T, SLOTS, Q, E, Z, X = 512, 2048, 512, 128, 512, 1024, 1024
FLOPS = 2 * D * Q * SLOTS + 2 * D * Q * Z + 2 * 2 * SLOTS * Q * E

F32 = mybir.dt.float32
BF16 = mybir.dt.bfloat16
I32 = mybir.dt.int32
U32 = mybir.dt.uint32
U16 = mybir.dt.uint16
U8 = mybir.dt.uint8
FP8X4 = mybir.dt.float8_e4m3fn_x4
ACT = mybir.ActivationFunctionType
ALU = mybir.AluOpType

P = 128
PACK = 4
BANK = 512
E_BLOCKS = E // P
LIST_COLS = SLOTS // 16
VEC_COLS = 320
LAST_VEC_LIST_COLS = 18


def tile_attend_widelarger_twostores_lean_kernel(
    tc, query, query2, keys_words, keys_scales, pages, factor1, factor2, vals, vals2, offs, offs2, offs3, out
):
    nc = tc.nc
    with ExitStack() as ctx:
        keep = ctx.enter_context(tc.tile_pool(name="keep", bufs=1))
        shared = ctx.enter_context(tc.tile_pool(name="shared", bufs=1))
        psum = ctx.enter_context(tc.psum_pool(name="psum", bufs=1))

        def sbuf(name, shape, dtype):
            return keep.tile(shape, dtype, name=name, tag=name, align_bytes=64)

        def load(name, shape, dtype, source):
            tile = sbuf(name, shape, dtype)
            nc.sync.dma_start(tile[:], source)
            return tile

        def by_fours(dst, src):
            return dst.rearrange("p (c i) t -> p c t i", i=4), src.rearrange("p t (c i) -> p c t i", i=4)

        def quantize(name, grouped, width):
            codes = sbuf(name + "_codes", [P, width], U32)
            scales = sbuf(name + "_scales", [P, width], U8)
            nc.vector.quantize_mx(out=codes[:].bitcast(FP8X4), scales=scales[:], in_=grouped)
            return codes, scales

        def product(acc, lhs, lhs_cols, rhs, rhs_cols, start, stop):
            nc.tensor.matmul_mx(
                out=acc,
                lhsT=lhs[0][:, lhs_cols].bitcast(FP8X4),
                lhsT_scale=lhs[1][:, lhs_cols],
                rhs=rhs[0][:, rhs_cols].bitcast(FP8X4),
                rhs_scale=rhs[1][:, rhs_cols],
                start=start,
                stop=stop,
            )

        key_scales = sbuf("key_scales", [P, T], U8)
        nc.gpsimd.memset(key_scales[:].bitcast(I32), 0)
        identity = sbuf("identity", [P, P], F32)
        make_identity(nc, identity[:])

        pages_by_k = pages.rearrange("(p t) z -> p t z", t=PACK)
        query2_raw = load("query2_raw", [P, PACK, Q], F32, query2.rearrange("(p t) q -> p t q", t=PACK))
        pages_raw = [
            load("pages_raw%d" % h, [P, PACK, BANK], F32, pages_by_k[:, :, h * BANK : (h + 1) * BANK])
            for h in range(Z // BANK)
        ]
        token_list = load("token_list", [P, LIST_COLS], U16, offs)
        query_raw = load("query_raw", [P, PACK, Q], F32, query.rearrange("(p t) q -> p t q", t=PACK))
        for row in range(4):
            nc.sync.dma_start(
                out=key_scales[row:P:32, :].bitcast(I32), in_=keys_scales[0, row:16:4, :].bitcast(I32)
            )
        key_words = sbuf("key_words", [P, T], U32)
        nc.sync.dma_start(
            out=key_words[:].bitcast(I32), in_=keys_words[0].rearrange("p n t -> p (n t)").bitcast(I32)
        )
        page_list = load("page_list", [P, LIST_COLS], U16, offs2)
        column_list = load("column_list", [P, LIST_COLS], U16, offs3)
        stores = []
        factors = []
        for j in range(E_BLOCKS):
            rows = slice(j * P, (j + 1) * P)
            store2 = load("store2_%d" % j, [P, X], F32, vals2[rows, :])
            if j < E_BLOCKS - 1:
                store1 = load("store1_%d" % j, [P, T], F32, vals[rows, :])
            else:
                store1 = shared.tile([P, T], F32, name="last_store1", align_bytes=64, offset=0)
                nc.sync.dma_start(store1[:], vals[rows, :])
            stores.append((store2, store1))
            if j == 0:
                for n, factor in enumerate((factor2, factor1)):
                    factors.append(load("factor%d" % n, [P, PACK], F32, factor[0].rearrange("(p t) -> p t", t=PACK)))

        def quantize_queries(name, raw):
            grouped = sbuf(name + "_grouped", [P, Q, PACK], BF16)
            nc.scalar.copy(*by_fours(grouped[:], raw[:]))
            return quantize(name, grouped[:].rearrange("p q t -> p (q t)"), Q)

        query2_mx = quantize_queries("query2", query2_raw)
        page_scores = sbuf("page_scores", [P, Z], F32)

        def score_pages(h):
            grouped = sbuf("pages_grouped%d" % h, [P, BANK, PACK], BF16)
            nc.vector.tensor_copy(*by_fours(grouped[:, 0:VEC_COLS, :], pages_raw[h][:, :, 0:VEC_COLS]))
            nc.scalar.copy(*by_fours(grouped[:, VEC_COLS:BANK, :], pages_raw[h][:, :, VEC_COLS:BANK]))
            pages_mx = quantize("pages%d" % h, grouped[:].rearrange("p z t -> p (z t)"), BANK)
            bank = psum.tile([P, BANK], F32, name="page_bank%d" % h)
            product(bank[:], query2_mx, slice(0, Q), pages_mx, slice(0, BANK), True, True)
            nc.scalar.copy(out=page_scores[:, h * BANK : (h + 1) * BANK], in_=bank[:])

        score_pages(0)
        score_pages(1)
        query_mx = quantize_queries("query", query_raw)
        picked_scales = sbuf("picked_scales", [P, SLOTS], U8)
        nc.vector.tensor_copy(picked_scales[:], key_scales[:].indirect(token_list[:]))
        picked_words = sbuf("picked_words", [P, SLOTS], U32)
        nc.vector.tensor_copy(picked_words[:], key_words[:].indirect(token_list[:]))
        picked_page_scores = sbuf("picked_page_scores", [P, SLOTS], F32)
        nc.scalar.activation(picked_page_scores[:], page_scores[:].indirect(page_list[:]), ACT.Copy)

        token_bank = psum.tile([P, SLOTS], F32, name="token_bank")
        product(token_bank[:], query_mx, slice(0, Q), (picked_words, picked_scales), slice(0, SLOTS), True, True)

        scores = sbuf("store2_0", [P, SLOTS], F32)
        nc.vector.tensor_tensor(scores[:], token_bank[:], picked_page_scores[:], ALU.max)
        weights = sbuf("weights", [P, PACK, P], F32)
        nc.scalar.activation(
            weights[:].rearrange("q t (c i) -> q c t i", i=4),
            scores[:].rearrange("q (c i t) -> q c t i", i=4, t=PACK),
            ACT.Sigmoid,
        )
        weight_bank = psum.tile([P, PACK, Q], F32, name="weight_bank")
        for t in range(PACK):
            nc.tensor.transpose(weight_bank[:, t, :], weights[:, t, :], identity[:])
        weights_grouped = sbuf("store2_1", [P, 2, Q, PACK], BF16)
        for n in range(2):
            nc.vector.tensor_tensor(
                weights_grouped[:, n, :, :],
                weight_bank[:].rearrange("p t q -> p q t"),
                factors[n][:].unsqueeze(1).to_broadcast([P, Q, PACK]),
                ALU.mult,
            )
        weights_mx = quantize("weights", weights_grouped[:].rearrange("p n q t -> p (n q t)"), 2 * Q)

        last = E_BLOCKS - 1

        def turn(name, picked, words, copy):
            pairs = picked[:].bitcast(F32)
            turned = psum.tile([P, 2, P], F32, name=name + "_turned", tag="turned", bufs=2)
            for u in range(2):
                nc.tensor.transpose(turned[:, u, :], pairs[:, u : SLOTS // 2 : 2], identity[:])
            copy(out=words.bitcast(F32), in_=turned[:].rearrange("p u e -> p e u"))

        def pick_store2(j):
            picked = sbuf("picked2_%d" % j, [P, SLOTS], BF16)
            nc.vector.tensor_copy(picked[:], stores[j][0][:].indirect(column_list[:]))
            return picked

        early_bank = psum.tile([P, last * P], F32, name="early_bank")
        for blocks in ((0, 1), (2,)):
            grouped = sbuf("grouped%d" % blocks[0], [P, len(blocks), 2, P, PACK], BF16)
            for place, j in enumerate(blocks):
                turn("values2_%d" % j, pick_store2(j), grouped[:, place, 0, :, :], nc.vector.tensor_copy)
                picked1 = sbuf("picked1_%d" % j, [P, SLOTS], BF16)
                nc.scalar.activation(picked1[:], stores[j][1][:].indirect(token_list[:]), ACT.Copy)
                turn("values1_%d" % j, picked1, grouped[:, place, 1, :, :], nc.scalar.copy)
            width = len(blocks) * 2 * P
            codes = sbuf("store2_%d" % (blocks[-1] + 1), [P, width], U32)
            scales = sbuf("scales%d" % blocks[0], [P, width], U8)
            nc.vector.quantize_mx(
                out=codes[:].bitcast(FP8X4), scales=scales[:], in_=grouped[:].rearrange("p j n e t -> p (j n e t)")
            )
            for place, j in enumerate(blocks):
                for n in range(2):
                    cols = slice((2 * place + n) * P, (2 * place + n + 1) * P)
                    acc = early_bank[:, j * P : (j + 1) * P]
                    product(acc, weights_mx, slice(n * Q, (n + 1) * Q), (codes, scales), cols, n == 0, n == 1)

        picked2 = pick_store2(last)
        picked1 = sbuf("picked1_%d" % last, [P, SLOTS], BF16)
        cut = 16 * LAST_VEC_LIST_COLS
        window = stores[last][1]
        nc.vector.tensor_copy(picked1[:, 0:cut], window[:].indirect(token_list[:, 0:LAST_VEC_LIST_COLS]))
        nc.scalar.activation(
            picked1[:, cut:SLOTS], window[:].indirect(token_list[:, LAST_VEC_LIST_COLS:LIST_COLS]), ACT.Copy
        )
        last_grouped2 = shared.tile([P, P, PACK], BF16, name="last_grouped2", align_bytes=64, offset=0)
        turn("values2_%d" % last, picked2, last_grouped2[:], nc.vector.tensor_copy)
        last_values2 = quantize("last_values2", last_grouped2[:].rearrange("p e t -> p (e t)"), P)
        early_result = shared.tile([P, last * P], F32, name="early_result", align_bytes=64, offset=2 * PACK * P)
        nc.scalar.copy(out=early_result[:], in_=early_bank[:])
        nc.sync.dma_start(out=out[:, 0 : last * P], in_=early_result[:])

        last_grouped1 = sbuf("last_grouped1", [P, P, PACK], BF16)
        turn("values1_%d" % last, picked1, last_grouped1[:], nc.scalar.copy)
        last_values1 = quantize("last_values1", last_grouped1[:].rearrange("p e t -> p (e t)"), P)
        last_bank = psum.tile([P, P], F32, name="last_bank")
        product(last_bank[:], weights_mx, slice(0, Q), last_values2, slice(0, P), True, False)
        product(last_bank[:], weights_mx, slice(Q, 2 * Q), last_values1, slice(0, P), False, True)
        last_result = sbuf("last_result", [P, P], F32)
        nc.scalar.copy(out=last_result[:], in_=last_bank[:])
        nc.scalar.dma_start(out=out[:, last * P : E], in_=last_result[:])
